import numpy as np
import ml_dtypes


def mxq(x, axis, fmt="e4m3"):
    dtype, down = {"e4m3": (ml_dtypes.float8_e4m3fn, 7), "e5m2": (ml_dtypes.float8_e5m2, 14)}[fmt]
    v = np.moveaxis(np.asarray(x, np.float32).astype(ml_dtypes.bfloat16).astype(np.float64), axis, -1)
    blocks = v.reshape(v.shape[:-1] + (-1, 32))
    amax = np.abs(blocks).max(-1, keepdims=True)
    byte = np.maximum(np.where(amax > 0, np.frexp(amax)[1] - 1 + 127, 0) - down, 1)
    scale = np.exp2(byte - 127.0)
    codes = (blocks / scale).astype(np.float32).astype(dtype).astype(np.float64)
    return np.moveaxis((codes * scale).reshape(v.shape), -1, axis)


WIDE = False


def mx_kscale(k):
    if not WIDE:
        return np.ones(k)
    levels = np.array([30, -30])
    if k % 512:
        return np.exp2(np.random.permutation(np.resize(levels, k // 32))).repeat(32)
    a = np.empty((k // 512, 16))
    for p in range(k // 512):
        a[p, :8] = np.random.permutation(np.resize(levels, 8))
        for g in range(8):
            far = levels[np.abs(levels - a[p, g]) >= 10]
            a[p, g + 8] = far[np.random.randint(len(far))]
    return np.exp2(a.ravel()).repeat(32)


def f64(x):
    return np.asarray(x).astype(np.float64)


def striped(idx):
    return np.tile(np.asarray(idx).reshape(-1, 16).T, (8, 1)).astype(np.uint16)


def unstriped(offs):
    return offs[:16].T.reshape(-1).astype(np.int64)


E2M1 = np.array([0.0, 0.5, 1.0, 1.5, 2.0, 3.0, 4.0, 6.0, -0.0, -0.5, -1.0, -1.5, -2.0, -3.0, -4.0, -6.0])


def pack_weight(w, fmt):
    k, n = w.shape
    w = f64(np.asarray(w, np.float32).astype(ml_dtypes.bfloat16)).reshape(k // 32, 32, n)
    amax = np.abs(w).max(1)
    if fmt in ("e4m3", "e5m2"):
        byte = np.frexp(amax)[1] - 1 + 127 - (7 if fmt == "e4m3" else 14)
    else:
        mant, ex = np.frexp(amax / 6.0)
        byte = np.where(mant > 0.5, ex, ex - 1) + 127
    byte = np.clip(np.where(amax > 0, byte, 1), 1, 254)
    scaled = (w * np.exp2(127.0 - byte)[:, None, :]).reshape(k, n).astype(np.float32)
    by_word = np.ascontiguousarray(scaled.reshape(k // 512, 128, 4, n).transpose(0, 1, 3, 2))
    if fmt in ("e4m3", "e5m2"):
        words = by_word.astype(ml_dtypes.float8_e4m3fn if fmt == "e4m3" else ml_dtypes.float8_e5m2).view(np.uint8)
    else:
        c = by_word.astype(ml_dtypes.float4_e2m1fn).view(np.uint8) & 0xF
        words = (c[..., 0::2] | (c[..., 1::2] << 4)).reshape(k // 512, 128, 2 * n)
    return np.ascontiguousarray(words), np.ascontiguousarray(byte.astype(np.uint8).reshape(k // 512, 16, n))


def unpack_weight(words, scales, fmt):
    g, _, n = scales.shape
    words = np.ascontiguousarray(words).reshape(g, 128, n, -1)
    if fmt in ("e4m3", "e5m2"):
        vals = words.view(ml_dtypes.float8_e4m3fn if fmt == "e4m3" else ml_dtypes.float8_e5m2).astype(np.float64)
    else:
        nib = np.empty((g, 128, n, 4), np.uint8)
        nib[..., 0::2] = words & 0xF
        nib[..., 1::2] = words >> 4
        vals = E2M1[nib]
    vals = vals * np.repeat(np.exp2(scales.astype(np.float64) - 127.0), 8, axis=1)[..., None]
    return vals.transpose(0, 1, 3, 2).reshape(g * 512, n)


K, T, J, N = 1024, 1024, 256, 256


def setup_inputs():
    n = np.random.standard_normal
    idx = np.random.permutation(T)[:J]
    idx2 = np.random.permutation(T)[:J]
    fk = mx_kscale(K)
    xtp = pack_weight(n((K, T)) * np.random.uniform(0.4, 1.6, (1, T)) / fk[:, None], "e5m2")
    wap = pack_weight(n((K, N)) * 1 / np.sqrt(K) * fk[:, None], "e4m3")
    return {
        "xt_words": xtp[0],
        "xt_scales": xtp[1],
        "wa_words": wap[0],
        "wa_scales": wap[1],
        "wb": (n((K, N)) * 1 / np.sqrt(K) * fk[:, None]).astype(np.float32),
        "bi": (np.random.uniform(-0.6, 0.6, (1, N))).astype(np.float32),
        "offs": striped(idx),
        "offs2": striped(idx2),
    }


def reference(xt_words, xt_scales, wa_words, wa_scales, wb, bi, offs, offs2):
    idx = unstriped(offs)
    idx2 = unstriped(offs2)
    xtu = unpack_weight(xt_words, xt_scales, "e5m2")
    wau = unpack_weight(wa_words, wa_scales, "e4m3")
    xtidxg = xtu[:, idx]
    a = xtidxg.T @ wau
    xtidx2g = xtu[:, idx2]
    wbq = mxq(f64(wb), 0, "e4m3")
    b0 = xtidx2g.T @ wbq
    b2 = b0 + f64(bi)
    ea = np.mean(np.square(a), axis=1, keepdims=True)
    eb = np.mean(np.square(b2), axis=1, keepdims=True)
    y = (a - b2) * (ea - eb)
    return y

@@ -1,0 +1,148 @@
+from contextlib import ExitStack
+
+import concourse.mybir as mybir
+from concourse.masks import make_identity
+
+K, T, J, N = 1024, 1024, 256, 256
+FLOPS = 2 * 2 * J * K * N
+
+F32 = mybir.dt.float32
+BF16 = mybir.dt.bfloat16
+I32 = mybir.dt.int32
+U32 = mybir.dt.uint32
+U16 = mybir.dt.uint16
+U8 = mybir.dt.uint8
+E4M3 = mybir.dt.float8_e4m3fn_x4
+E5M2 = mybir.dt.float8_e5m2_x4
+ALU = mybir.AluOpType
+ACT = mybir.ActivationFunctionType
+
+P = 128
+PACK = 4
+PASSES = K // (P * PACK)
+J_TILES = J // P
+SCALAR_COLS = (256, 192)
+
+
+def tile_list_rows_twotokens_energygap_kernel(tc, xt_words, xt_scales, wa_words, wa_scales, wb, bi, offs, offs2, out):
+    nc = tc.nc
+    with ExitStack() as ctx:
+        sb = ctx.enter_context(tc.tile_pool(name="sb", bufs=1))
+        ps = ctx.enter_context(tc.psum_pool(name="ps", bufs=1))
+
+        lists = [sb.tile([P, J // 16], U16, name=f"list{l}") for l in range(2)]
+        x_scales = sb.tile([P, PASSES, T], U8, align_bytes=64)
+        x_words = [sb.tile([P, T], I32, name=f"x_words{z}", align_bytes=64) for z in range(PASSES)]
+        wb_raw = [sb.tile([P, PACK, N], F32, name=f"wb_raw{z}", align_bytes=64) for z in range(PASSES)]
+        a_words = sb.tile([P, PASSES, N], I32, align_bytes=64)
+        a_scales = sb.tile([P, PASSES, N], U8, align_bytes=64)
+        bias_col = sb.tile([P, 2], F32)
+        identity = sb.tile([P, P], F32)
+
+        nc.vector.memset(x_scales[:].bitcast(I32), 0)
+        nc.gpsimd.dma_start(out=bias_col[:], in_=bi.rearrange("o (p q) -> (o p) q", q=2))
+        make_identity(nc, identity[:])
+        nc.gpsimd.memset(a_scales[:].bitcast(I32), 0)
+
+        def load_scales(queue, tile, src):
+            for q in range(4):
+                queue.dma_start(
+                    out=tile[32 * q : 32 * q + 4, :, :].bitcast(I32),
+                    in_=src[:, 4 * q : 4 * q + 4, :].rearrange("z r c -> r z c").bitcast(I32),
+                )
+
+        def load_x(z):
+            nc.sync.dma_start(out=x_words[z][:], in_=xt_words[z].rearrange("p c r -> p (c r)").bitcast(I32))
+
+        def load_wb(z):
+            rows = wb[z * P * PACK : (z + 1) * P * PACK, :]
+            nc.sync.dma_start(out=wb_raw[z][:], in_=rows.rearrange("(p t) n -> p t n", t=PACK))
+
+        nc.sync.dma_start(lists[0][:], offs)
+        nc.sync.dma_start(lists[1][:], offs2)
+        load_scales(nc.scalar, x_scales, xt_scales)
+        load_wb(0)
+        load_x(0)
+        load_wb(1)
+        load_x(1)
+        nc.sync.dma_start(out=a_words[:], in_=wa_words.rearrange("z p c r -> p z (c r)").bitcast(I32))
+        load_scales(nc.sync, a_scales, wa_scales)
+
+        bias_ps = ps.tile([P, 2, P], F32)
+        for q in range(2):
+            nc.tensor.transpose(bias_ps[:, q, :], bias_col[:, q : q + 1].to_broadcast([P, P]), identity[:])
+        bias = sb.tile([P, N], F32)
+        nc.scalar.activation(
+            out=bias[:].rearrange("p (c q) -> p c q", q=2), in_=bias_ps[:].rearrange("p q c -> p c q"), func=ACT.Copy
+        )
+
+        g_scales = [[sb.tile([P, J], U8, name=f"g_scales{l}{z}", align_bytes=64) for z in range(PASSES)] for l in range(2)]
+        g_words = [[sb.tile([P, J], U32, name=f"g_words{l}{z}", align_bytes=64) for z in range(PASSES)] for l in range(2)]
+        wb_bf = [sb.tile([P, N, PACK], BF16, name=f"wb_bf{z}", align_bytes=64) for z in range(PASSES)]
+        b_words = [sb.tile([P, N], U32, name=f"b_words{z}", align_bytes=64) for z in range(PASSES)]
+        b_scales = [sb.tile([P, N], U8, name=f"b_scales{z}", align_bytes=64) for z in range(PASSES)]
+        acc = [[ps.tile([P, N], F32, name=f"acc{l}{h}") for h in range(J_TILES)] for l in range(2)]
+
+        def round_views(z, c0, c1):
+            dst = wb_bf[z][:, c0:c1, :].rearrange("p (c i) t -> p c t i", i=4)
+            src = wb_raw[z][:, :, c0:c1].rearrange("p t (c i) -> p c t i", i=4)
+            return dst, src
+
+        def gather_words(l, z):
+            nc.vector.tensor_copy(g_words[l][z][:], x_words[z][:].bitcast(U32).indirect(lists[l][:]))
+
+        def quantize(z):
+            nc.vector.quantize_mx(
+                out=b_words[z][:].bitcast(E4M3), scales=b_scales[z][:], in_=wb_bf[z][:].rearrange("p n t -> p (n t)")
+            )
+
+        def multiply(l, z):
+            words = a_words[:, z, :] if l == 0 else b_words[z][:]
+            scales = a_scales[:, z, :] if l == 0 else b_scales[z][:]
+            for h in range(J_TILES):
+                cols = slice(h * P, (h + 1) * P)
+                nc.tensor.matmul_mx(
+                    out=acc[l][h][:],
+                    lhsT=g_words[l][z][:, cols].bitcast(E5M2),
+                    lhsT_scale=g_scales[l][z][:, cols],
+                    rhs=words.bitcast(E4M3),
+                    rhs_scale=scales,
+                    start=(z == 0),
+                    stop=(z == PASSES - 1),
+                )
+
+        for z in range(PASSES):
+            for l in range(2):
+                nc.vector.tensor_copy(g_scales[l][z][:], x_scales[:, z, :].indirect(lists[l][:]))
+
+        for z in range(PASSES):
+            dst, src = round_views(z, 0, SCALAR_COLS[z])
+            nc.scalar.activation(out=dst, in_=src, func=ACT.Copy)
+            if SCALAR_COLS[z] < N:
+                dst, src = round_views(z, SCALAR_COLS[z], N)
+                nc.vector.tensor_copy(out=dst, in_=src)
+            gather_words(0, z)
+            gather_words(1, z)
+            quantize(z)
+        multiply(1, 0)
+        multiply(0, 0)
+        multiply(0, 1)
+        multiply(1, 1)
+
+        squares = sb.tile([P, N], F32)
+        energy = [[sb.tile([P, 1], F32, name=f"energy{l}{h}") for h in range(J_TILES)] for l in range(2)]
+        for h in range(J_TILES):
+            nc.scalar.activation(out=squares[:], in_=acc[0][h][:], func=ACT.Square, scale=1.0 / 16, accum_out=energy[0][h][:])
+        b2 = [sb.tile([P, N], F32, name=f"b2_{h}") for h in range(J_TILES)]
+        gap = [sb.tile([P, N], F32, name=f"gap{h}") for h in range(J_TILES)]
+        egap = [sb.tile([P, 1], F32, name=f"egap{h}") for h in range(J_TILES)]
+        res = [sb.tile([P, N], F32, name=f"res{h}") for h in range(J_TILES)]
+        for h in range(J_TILES):
+            nc.vector.tensor_tensor(b2[h][:], acc[1][h][:], bias[:], ALU.add)
+        for h in range(J_TILES):
+            nc.scalar.activation(out=squares[:], in_=b2[h][:], func=ACT.Square, scale=1.0 / 16, accum_out=energy[1][h][:])
+            nc.scalar.activation(out=egap[h][:], in_=energy[1][h][:], func=ACT.Identity, scale=-1.0, bias=energy[0][h][:])
+            nc.vector.tensor_tensor(gap[h][:], acc[0][h][:], b2[h][:], ALU.subtract)
+        for h in range(J_TILES):
+            nc.vector.tensor_scalar(res[h][:], gap[h][:], egap[h][:], None, ALU.mult)
+            nc.sync.dma_start(out=out[h * P : (h + 1) * P, :], in_=res[h][:])

@@ -21,7 +21,6 @@ P = 128
 PACK = 4
 PASSES = K // (P * PACK)
 J_TILES = J // P
-SCALAR_COLS = (256, 192)
 
 
 def tile_list_rows_twotokens_energygap_kernel(tc, xt_words, xt_scales, wa_words, wa_scales, wb, bi, offs, offs2, out):
@@ -31,42 +30,51 @@ def tile_list_rows_twotokens_energygap_kernel(tc, xt_words, xt_scales, wa_words,
         ps = ctx.enter_context(tc.psum_pool(name="ps", bufs=1))
 
         lists = [sb.tile([P, J // 16], U16, name=f"list{l}") for l in range(2)]
-        x_scales = sb.tile([P, PASSES, T], U8, align_bytes=64)
+        x_scales = sb.tile([P, T], U8, align_bytes=64)
+        moved = sb.tile([P, 2, J], U8, align_bytes=64)
         x_words = [sb.tile([P, T], I32, name=f"x_words{z}", align_bytes=64) for z in range(PASSES)]
         wb_raw = [sb.tile([P, PACK, N], F32, name=f"wb_raw{z}", align_bytes=64) for z in range(PASSES)]
-        a_words = sb.tile([P, PASSES, N], I32, align_bytes=64)
+        a_words = [sb.tile([P, N], I32, name=f"a_words{z}", align_bytes=64) for z in range(PASSES)]
         a_scales = sb.tile([P, PASSES, N], U8, align_bytes=64)
         bias_col = sb.tile([P, 2], F32)
         identity = sb.tile([P, P], F32)
 
         nc.vector.memset(x_scales[:].bitcast(I32), 0)
-        nc.gpsimd.dma_start(out=bias_col[:], in_=bi.rearrange("o (p q) -> (o p) q", q=2))
-        make_identity(nc, identity[:])
-        nc.gpsimd.memset(a_scales[:].bitcast(I32), 0)
+        nc.vector.memset(a_scales[:].bitcast(I32), 0)
+        nc.vector.memset(moved[:].bitcast(I32), 0)
 
-        def load_scales(queue, tile, src):
-            for q in range(4):
-                queue.dma_start(
-                    out=tile[32 * q : 32 * q + 4, :, :].bitcast(I32),
-                    in_=src[:, 4 * q : 4 * q + 4, :].rearrange("z r c -> r z c").bitcast(I32),
-                )
+        def load_a_scales(queue, q):
+            queue.dma_start(
+                out=a_scales[32 * q : 32 * q + 4, :, :].bitcast(I32),
+                in_=wa_scales[:, 4 * q : 4 * q + 4, :].rearrange("z r c -> r z c").bitcast(I32),
+            )
 
         def load_x(z):
             nc.sync.dma_start(out=x_words[z][:], in_=xt_words[z].rearrange("p c r -> p (c r)").bitcast(I32))
+
+        def load_a(z):
+            nc.sync.dma_start(out=a_words[z][:], in_=wa_words[z].rearrange("p c r -> p (c r)").bitcast(I32))
 
         def load_wb(z):
             rows = wb[z * P * PACK : (z + 1) * P * PACK, :]
             nc.sync.dma_start(out=wb_raw[z][:], in_=rows.rearrange("(p t) n -> p t n", t=PACK))
 
+        nc.gpsimd.dma_start(out=bias_col[:], in_=bi.rearrange("o (p q) -> (o p) q", q=2))
+        make_identity(nc, identity[:])
+
         nc.sync.dma_start(lists[0][:], offs)
         nc.sync.dma_start(lists[1][:], offs2)
-        load_scales(nc.scalar, x_scales, xt_scales)
-        load_wb(0)
+        by_row = xt_scales.rearrange("z (q r) c -> r q z c", r=4)
+        for r, queue in enumerate((nc.sync, nc.scalar, nc.sync, nc.scalar)):
+            queue.dma_start(out=x_scales[r:P:16, :].bitcast(I32), in_=by_row[r].bitcast(I32))
         load_x(0)
-        load_wb(1)
+        load_wb(0)
+        for q in range(4):
+            load_a_scales(nc.sync, q)
         load_x(1)
-        nc.sync.dma_start(out=a_words[:], in_=wa_words.rearrange("z p c r -> p z (c r)").bitcast(I32))
-        load_scales(nc.sync, a_scales, wa_scales)
+        load_wb(1)
+        load_a(0)
+        load_a(1)
 
         bias_ps = ps.tile([P, 2, P], F32)
         for q in range(2):
@@ -76,7 +84,7 @@ def tile_list_rows_twotokens_energygap_kernel(tc, xt_words, xt_scales, wa_words,
             out=bias[:].rearrange("p (c q) -> p c q", q=2), in_=bias_ps[:].rearrange("p q c -> p c q"), func=ACT.Copy
         )
 
-        g_scales = [[sb.tile([P, J], U8, name=f"g_scales{l}{z}", align_bytes=64) for z in range(PASSES)] for l in range(2)]
+        g_scales = sb.tile([P, 2, J], U8, align_bytes=64)
         g_words = [[sb.tile([P, J], U32, name=f"g_words{l}{z}", align_bytes=64) for z in range(PASSES)] for l in range(2)]
         wb_bf = [sb.tile([P, N, PACK], BF16, name=f"wb_bf{z}", align_bytes=64) for z in range(PASSES)]
         b_words = [sb.tile([P, N], U32, name=f"b_words{z}", align_bytes=64) for z in range(PASSES)]
@@ -97,33 +105,42 @@ def tile_list_rows_twotokens_energygap_kernel(tc, xt_words, xt_scales, wa_words,
             )
 
         def multiply(l, z):
-            words = a_words[:, z, :] if l == 0 else b_words[z][:]
+            words = a_words[z][:] if l == 0 else b_words[z][:]
             scales = a_scales[:, z, :] if l == 0 else b_scales[z][:]
             for h in range(J_TILES):
                 cols = slice(h * P, (h + 1) * P)
                 nc.tensor.matmul_mx(
                     out=acc[l][h][:],
                     lhsT=g_words[l][z][:, cols].bitcast(E5M2),
-                    lhsT_scale=g_scales[l][z][:, cols],
+                    lhsT_scale=(g_scales, moved)[z][:, l, cols],
                     rhs=words.bitcast(E4M3),
                     rhs_scale=scales,
                     start=(z == 0),
                     stop=(z == PASSES - 1),
                 )
 
-        for z in range(PASSES):
-            for l in range(2):
-                nc.vector.tensor_copy(g_scales[l][z][:], x_scales[:, z, :].indirect(lists[l][:]))
+        for l in range(2):
+            nc.vector.tensor_copy(g_scales[:, l, :], x_scales[:].indirect(lists[l][:]))
+        for q in range(4):
+            nc.sync.dma_start(
+                out=moved[32 * q : 32 * q + 4, :, :].bitcast(I32), in_=g_scales[32 * q + 16 : 32 * q + 20, :, :].bitcast(I32)
+            )
 
-        for z in range(PASSES):
-            dst, src = round_views(z, 0, SCALAR_COLS[z])
+        def round_wb(z, split):
+            dst, src = round_views(z, 0, split)
             nc.scalar.activation(out=dst, in_=src, func=ACT.Copy)
-            if SCALAR_COLS[z] < N:
-                dst, src = round_views(z, SCALAR_COLS[z], N)
+            if split < N:
+                dst, src = round_views(z, split, N)
                 nc.vector.tensor_copy(out=dst, in_=src)
-            gather_words(0, z)
-            gather_words(1, z)
-            quantize(z)
+
+        gather_words(1, 0)
+        gather_words(0, 0)
+        round_wb(0, 192)
+        quantize(0)
+        gather_words(0, 1)
+        gather_words(1, 1)
+        round_wb(1, 160)
+        quantize(1)
         multiply(1, 0)
         multiply(0, 0)
         multiply(0, 1)
@@ -131,18 +148,19 @@ def tile_list_rows_twotokens_energygap_kernel(tc, xt_words, xt_scales, wa_words,
 
         squares = sb.tile([P, N], F32)
         energy = [[sb.tile([P, 1], F32, name=f"energy{l}{h}") for h in range(J_TILES)] for l in range(2)]
-        for h in range(J_TILES):
-            nc.scalar.activation(out=squares[:], in_=acc[0][h][:], func=ACT.Square, scale=1.0 / 16, accum_out=energy[0][h][:])
         b2 = [sb.tile([P, N], F32, name=f"b2_{h}") for h in range(J_TILES)]
         gap = [sb.tile([P, N], F32, name=f"gap{h}") for h in range(J_TILES)]
         egap = [sb.tile([P, 1], F32, name=f"egap{h}") for h in range(J_TILES)]
         res = [sb.tile([P, N], F32, name=f"res{h}") for h in range(J_TILES)]
+        for h in range(J_TILES):
+            nc.scalar.activation(out=squares[:], in_=acc[0][h][:], func=ACT.Square, scale=1.0 / 16, accum_out=energy[0][h][:])
         for h in range(J_TILES):
             nc.vector.tensor_tensor(b2[h][:], acc[1][h][:], bias[:], ALU.add)
         for h in range(J_TILES):
             nc.scalar.activation(out=squares[:], in_=b2[h][:], func=ACT.Square, scale=1.0 / 16, accum_out=energy[1][h][:])
             nc.scalar.activation(out=egap[h][:], in_=energy[1][h][:], func=ACT.Identity, scale=-1.0, bias=energy[0][h][:])
             nc.vector.tensor_tensor(gap[h][:], acc[0][h][:], b2[h][:], ALU.subtract)
-        for h in range(J_TILES):
-            nc.vector.tensor_scalar(res[h][:], gap[h][:], egap[h][:], None, ALU.mult)
-            nc.sync.dma_start(out=out[h * P : (h + 1) * P, :], in_=res[h][:])
+        nc.scalar.activation(out=res[0][:], in_=gap[0][:], func=ACT.Copy, scale=egap[0][:])
+        nc.scalar.dma_start(out=out[0:P, :], in_=res[0][:])
+        nc.vector.tensor_scalar(res[1][:], gap[1][:], egap[1][:], None, ALU.mult)
+        nc.sync.dma_start(out=out[P : 2 * P, :], in_=res[1][:])

@@ -63,17 +63,17 @@ def tile_list_rows_twotokens_energygap_kernel(tc, xt_words, xt_scales, wa_words,
         make_identity(nc, identity[:])
 
         nc.sync.dma_start(lists[0][:], offs)
-        nc.sync.dma_start(lists[1][:], offs2)
         by_row = xt_scales.rearrange("z (q r) c -> r q z c", r=4)
         for r, queue in enumerate((nc.sync, nc.scalar, nc.sync, nc.scalar)):
             queue.dma_start(out=x_scales[r:P:16, :].bitcast(I32), in_=by_row[r].bitcast(I32))
+        nc.sync.dma_start(lists[1][:], offs2)
         load_x(0)
         load_wb(0)
         for q in range(4):
             load_a_scales(nc.sync, q)
-        load_x(1)
-        load_wb(1)
         load_a(0)
+        load_wb(1)
+        load_x(1)
         load_a(1)
 
         bias_ps = ps.tile([P, 2, P], F32)
@@ -104,10 +104,10 @@ def tile_list_rows_twotokens_energygap_kernel(tc, xt_words, xt_scales, wa_words,
                 out=b_words[z][:].bitcast(E4M3), scales=b_scales[z][:], in_=wb_bf[z][:].rearrange("p n t -> p (n t)")
             )
 
-        def multiply(l, z):
+        def multiply(l, z, tiles):
             words = a_words[z][:] if l == 0 else b_words[z][:]
             scales = a_scales[:, z, :] if l == 0 else b_scales[z][:]
-            for h in range(J_TILES):
+            for h in tiles:
                 cols = slice(h * P, (h + 1) * P)
                 nc.tensor.matmul_mx(
                     out=acc[l][h][:],
@@ -137,29 +137,44 @@ def tile_list_rows_twotokens_energygap_kernel(tc, xt_words, xt_scales, wa_words,
         gather_words(0, 0)
         round_wb(0, 192)
         quantize(0)
-        gather_words(0, 1)
-        gather_words(1, 1)
-        round_wb(1, 160)
+        round_wb(1, 112)
         quantize(1)
-        multiply(1, 0)
-        multiply(0, 0)
-        multiply(0, 1)
-        multiply(1, 1)
+        for h in range(J_TILES):
+            for l in (1, 0):
+                nc.vector.tensor_copy(
+                    g_words[l][1][:, h * P : (h + 1) * P], x_words[1][:].bitcast(U32).indirect(lists[l][:, 8 * h : 8 * h + 8])
+                )
+        multiply(0, 0, range(J_TILES))
+        multiply(1, 0, range(J_TILES))
+        for h in range(J_TILES):
+            multiply(1, 1, [h])
+            multiply(0, 1, [h])
 
-        squares = sb.tile([P, N], F32)
         energy = [[sb.tile([P, 1], F32, name=f"energy{l}{h}") for h in range(J_TILES)] for l in range(2)]
         b2 = [sb.tile([P, N], F32, name=f"b2_{h}") for h in range(J_TILES)]
         gap = [sb.tile([P, N], F32, name=f"gap{h}") for h in range(J_TILES)]
         egap = [sb.tile([P, 1], F32, name=f"egap{h}") for h in range(J_TILES)]
         res = [sb.tile([P, N], F32, name=f"res{h}") for h in range(J_TILES)]
         for h in range(J_TILES):
-            nc.scalar.activation(out=squares[:], in_=acc[0][h][:], func=ACT.Square, scale=1.0 / 16, accum_out=energy[0][h][:])
-        for h in range(J_TILES):
             nc.vector.tensor_tensor(b2[h][:], acc[1][h][:], bias[:], ALU.add)
-        for h in range(J_TILES):
-            nc.scalar.activation(out=squares[:], in_=b2[h][:], func=ACT.Square, scale=1.0 / 16, accum_out=energy[1][h][:])
+        def square_sum(k, src, dst):
+            squares = sb.tile([P, N], F32, name=f"squares{k}")
+            nc.scalar.activation(out=squares[:], in_=src[:], func=ACT.Square, scale=1.0 / 16, accum_out=dst[:])
+
+        def energy_gap(h):
             nc.scalar.activation(out=egap[h][:], in_=energy[1][h][:], func=ACT.Identity, scale=-1.0, bias=energy[0][h][:])
-            nc.vector.tensor_tensor(gap[h][:], acc[0][h][:], b2[h][:], ALU.subtract)
+
+        square_sum(0, acc[0][0], energy[0][0])
+        square_sum(1, b2[0], energy[1][0])
+        square_sum(2, acc[0][1], energy[0][1])
+        nc.vector.tensor_tensor(gap[0][:], acc[0][0][:], b2[0][:], ALU.subtract)
+        squares_v = sb.tile([P, N], F32)
+        nc.vector.scalar_tensor_tensor(
+            squares_v[:], b2[1][:], 1.0 / N, b2[1][:], ALU.mult, ALU.mult, accum_out=energy[1][1][:]
+        )
+        nc.vector.tensor_tensor(gap[1][:], acc[0][1][:], b2[1][:], ALU.subtract)
+        energy_gap(0)
+        energy_gap(1)
         nc.scalar.activation(out=res[0][:], in_=gap[0][:], func=ACT.Copy, scale=egap[0][:])
         nc.scalar.dma_start(out=out[0:P, :], in_=res[0][:])
         nc.vector.tensor_scalar(res[1][:], gap[1][:], egap[1][:], None, ALU.mult)

@@ -71,9 +71,9 @@ def tile_list_rows_twotokens_energygap_kernel(tc, xt_words, xt_scales, wa_words,
         load_wb(0)
         for q in range(4):
             load_a_scales(nc.sync, q)
-        load_a(0)
         load_wb(1)
         load_x(1)
+        load_a(0)
         load_a(1)
 
         bias_ps = ps.tile([P, 2, P], F32)
@@ -144,8 +144,8 @@ def tile_list_rows_twotokens_energygap_kernel(tc, xt_words, xt_scales, wa_words,
                 nc.vector.tensor_copy(
                     g_words[l][1][:, h * P : (h + 1) * P], x_words[1][:].bitcast(U32).indirect(lists[l][:, 8 * h : 8 * h + 8])
                 )
-        multiply(0, 0, range(J_TILES))
         multiply(1, 0, range(J_TILES))
+        multiply(0, 0, range(J_TILES))
         for h in range(J_TILES):
             multiply(1, 1, [h])
             multiply(0, 1, [h])
@@ -174,7 +174,7 @@ def tile_list_rows_twotokens_energygap_kernel(tc, xt_words, xt_scales, wa_words,
         )
         nc.vector.tensor_tensor(gap[1][:], acc[0][1][:], b2[1][:], ALU.subtract)
         energy_gap(0)
-        energy_gap(1)
+        nc.vector.tensor_tensor(egap[1][:], energy[0][1][:], energy[1][1][:], ALU.subtract)
         nc.scalar.activation(out=res[0][:], in_=gap[0][:], func=ACT.Copy, scale=egap[0][:])
         nc.scalar.dma_start(out=out[0:P, :], in_=res[0][:])
         nc.vector.tensor_scalar(res[1][:], gap[1][:], egap[1][:], None, ALU.mult)

from contextlib import ExitStack

import concourse.mybir as mybir
from concourse.masks import make_identity

K, T, J, N = 1024, 1024, 256, 256
FLOPS = 2 * 2 * J * K * N

F32 = mybir.dt.float32
BF16 = mybir.dt.bfloat16
I32 = mybir.dt.int32
U32 = mybir.dt.uint32
U16 = mybir.dt.uint16
U8 = mybir.dt.uint8
E4M3 = mybir.dt.float8_e4m3fn_x4
E5M2 = mybir.dt.float8_e5m2_x4
ALU = mybir.AluOpType
ACT = mybir.ActivationFunctionType

P = 128
PACK = 4
PASSES = K // (P * PACK)
J_TILES = J // P


def tile_list_rows_twotokens_energygap_kernel(tc, xt_words, xt_scales, wa_words, wa_scales, wb, bi, offs, offs2, out):
    nc = tc.nc
    with ExitStack() as ctx:
        sb = ctx.enter_context(tc.tile_pool(name="sb", bufs=1))
        ps = ctx.enter_context(tc.psum_pool(name="ps", bufs=1))

        lists = [sb.tile([P, J // 16], U16, name=f"list{l}") for l in range(2)]
        x_scales = sb.tile([P, T], U8, align_bytes=64)
        moved = sb.tile([P, 2, J], U8, align_bytes=64)
        x_words = [sb.tile([P, T], I32, name=f"x_words{z}", align_bytes=64) for z in range(PASSES)]
        wb_raw = [sb.tile([P, PACK, N], F32, name=f"wb_raw{z}", align_bytes=64) for z in range(PASSES)]
        a_words = [sb.tile([P, N], I32, name=f"a_words{z}", align_bytes=64) for z in range(PASSES)]
        a_scales = sb.tile([P, PASSES, N], U8, align_bytes=64)
        bias_col = sb.tile([P, 2], F32)
        identity = sb.tile([P, P], F32)

        nc.vector.memset(x_scales[:].bitcast(I32), 0)
        nc.vector.memset(a_scales[:].bitcast(I32), 0)
        nc.vector.memset(moved[:].bitcast(I32), 0)

        def load_a_scales(queue, q):
            queue.dma_start(
                out=a_scales[32 * q : 32 * q + 4, :, :].bitcast(I32),
                in_=wa_scales[:, 4 * q : 4 * q + 4, :].rearrange("z r c -> r z c").bitcast(I32),
            )

        def load_x(z):
            nc.sync.dma_start(out=x_words[z][:], in_=xt_words[z].rearrange("p c r -> p (c r)").bitcast(I32))

        def load_a(z):
            nc.sync.dma_start(out=a_words[z][:], in_=wa_words[z].rearrange("p c r -> p (c r)").bitcast(I32))

        def load_wb(z):
            rows = wb[z * P * PACK : (z + 1) * P * PACK, :]
            nc.sync.dma_start(out=wb_raw[z][:], in_=rows.rearrange("(p t) n -> p t n", t=PACK))

        nc.gpsimd.dma_start(out=bias_col[:], in_=bi.rearrange("o (p q) -> (o p) q", q=2))
        make_identity(nc, identity[:])

        nc.sync.dma_start(lists[0][:], offs)
        by_row = xt_scales.rearrange("z (q r) c -> r q z c", r=4)
        for r, queue in enumerate((nc.sync, nc.scalar, nc.sync, nc.scalar)):
            queue.dma_start(out=x_scales[r:P:16, :].bitcast(I32), in_=by_row[r].bitcast(I32))
        nc.sync.dma_start(lists[1][:], offs2)
        load_x(0)
        load_wb(0)
        for q in range(4):
            load_a_scales(nc.sync, q)
        load_wb(1)
        load_x(1)
        load_a(0)
        load_a(1)

        bias_ps = ps.tile([P, 2, P], F32)
        for q in range(2):
            nc.tensor.transpose(bias_ps[:, q, :], bias_col[:, q : q + 1].to_broadcast([P, P]), identity[:])
        bias = sb.tile([P, N], F32)
        nc.scalar.activation(
            out=bias[:].rearrange("p (c q) -> p c q", q=2), in_=bias_ps[:].rearrange("p q c -> p c q"), func=ACT.Copy
        )

        g_scales = sb.tile([P, 2, J], U8, align_bytes=64)
        g_words = [[sb.tile([P, J], U32, name=f"g_words{l}{z}", align_bytes=64) for z in range(PASSES)] for l in range(2)]
        wb_bf = [sb.tile([P, N, PACK], BF16, name=f"wb_bf{z}", align_bytes=64) for z in range(PASSES)]
        b_words = [sb.tile([P, N], U32, name=f"b_words{z}", align_bytes=64) for z in range(PASSES)]
        b_scales = [sb.tile([P, N], U8, name=f"b_scales{z}", align_bytes=64) for z in range(PASSES)]
        acc = [[ps.tile([P, N], F32, name=f"acc{l}{h}") for h in range(J_TILES)] for l in range(2)]

        def round_views(z, c0, c1):
            dst = wb_bf[z][:, c0:c1, :].rearrange("p (c i) t -> p c t i", i=4)
            src = wb_raw[z][:, :, c0:c1].rearrange("p t (c i) -> p c t i", i=4)
            return dst, src

        def gather_words(l, z):
            nc.vector.tensor_copy(g_words[l][z][:], x_words[z][:].bitcast(U32).indirect(lists[l][:]))

        def quantize(z):
            nc.vector.quantize_mx(
                out=b_words[z][:].bitcast(E4M3), scales=b_scales[z][:], in_=wb_bf[z][:].rearrange("p n t -> p (n t)")
            )

        def multiply(l, z, tiles):
            words = a_words[z][:] if l == 0 else b_words[z][:]
            scales = a_scales[:, z, :] if l == 0 else b_scales[z][:]
            for h in tiles:
                cols = slice(h * P, (h + 1) * P)
                nc.tensor.matmul_mx(
                    out=acc[l][h][:],
                    lhsT=g_words[l][z][:, cols].bitcast(E5M2),
                    lhsT_scale=(g_scales, moved)[z][:, l, cols],
                    rhs=words.bitcast(E4M3),
                    rhs_scale=scales,
                    start=(z == 0),
                    stop=(z == PASSES - 1),
                )

        for l in range(2):
            nc.vector.tensor_copy(g_scales[:, l, :], x_scales[:].indirect(lists[l][:]))
        for q in range(4):
            nc.sync.dma_start(
                out=moved[32 * q : 32 * q + 4, :, :].bitcast(I32), in_=g_scales[32 * q + 16 : 32 * q + 20, :, :].bitcast(I32)
            )

        def round_wb(z, split):
            dst, src = round_views(z, 0, split)
            nc.scalar.activation(out=dst, in_=src, func=ACT.Copy)
            if split < N:
                dst, src = round_views(z, split, N)
                nc.vector.tensor_copy(out=dst, in_=src)

        gather_words(1, 0)
        gather_words(0, 0)
        round_wb(0, 192)
        quantize(0)
        round_wb(1, 112)
        quantize(1)
        for h in range(J_TILES):
            for l in (1, 0):
                nc.vector.tensor_copy(
                    g_words[l][1][:, h * P : (h + 1) * P], x_words[1][:].bitcast(U32).indirect(lists[l][:, 8 * h : 8 * h + 8])
                )
        multiply(1, 0, range(J_TILES))
        multiply(0, 0, range(J_TILES))
        for h in range(J_TILES):
            multiply(1, 1, [h])
            multiply(0, 1, [h])

        energy = [[sb.tile([P, 1], F32, name=f"energy{l}{h}") for h in range(J_TILES)] for l in range(2)]
        b2 = [sb.tile([P, N], F32, name=f"b2_{h}") for h in range(J_TILES)]
        gap = [sb.tile([P, N], F32, name=f"gap{h}") for h in range(J_TILES)]
        egap = [sb.tile([P, 1], F32, name=f"egap{h}") for h in range(J_TILES)]
        res = [sb.tile([P, N], F32, name=f"res{h}") for h in range(J_TILES)]
        for h in range(J_TILES):
            nc.vector.tensor_tensor(b2[h][:], acc[1][h][:], bias[:], ALU.add)
        def square_sum(k, src, dst):
            squares = sb.tile([P, N], F32, name=f"squares{k}")
            nc.scalar.activation(out=squares[:], in_=src[:], func=ACT.Square, scale=1.0 / 16, accum_out=dst[:])

        def energy_gap(h):
            nc.scalar.activation(out=egap[h][:], in_=energy[1][h][:], func=ACT.Identity, scale=-1.0, bias=energy[0][h][:])

        square_sum(0, acc[0][0], energy[0][0])
        square_sum(1, b2[0], energy[1][0])
        square_sum(2, acc[0][1], energy[0][1])
        nc.vector.tensor_tensor(gap[0][:], acc[0][0][:], b2[0][:], ALU.subtract)
        squares_v = sb.tile([P, N], F32)
        nc.vector.scalar_tensor_tensor(
            squares_v[:], b2[1][:], 1.0 / N, b2[1][:], ALU.mult, ALU.mult, accum_out=energy[1][1][:]
        )
        nc.vector.tensor_tensor(gap[1][:], acc[0][1][:], b2[1][:], ALU.subtract)
        energy_gap(0)
        nc.vector.tensor_tensor(egap[1][:], energy[0][1][:], energy[1][1][:], ALU.subtract)
        nc.scalar.activation(out=res[0][:], in_=gap[0][:], func=ACT.Copy, scale=egap[0][:])
        nc.scalar.dma_start(out=out[0:P, :], in_=res[0][:])
        nc.vector.tensor_scalar(res[1][:], gap[1][:], egap[1][:], None, ALU.mult)
        nc.sync.dma_start(out=out[P : 2 * P, :], in_=res[1][:])
